import numpy as np
import ml_dtypes


def mxq(x, axis, fmt="e4m3"):
    dtype, down = {"e4m3": (ml_dtypes.float8_e4m3fn, 7), "e5m2": (ml_dtypes.float8_e5m2, 14)}[fmt]
    v = np.moveaxis(np.asarray(x, np.float32).astype(ml_dtypes.bfloat16).astype(np.float64), axis, -1)
    blocks = v.reshape(v.shape[:-1] + (-1, 32))
    amax = np.abs(blocks).max(-1, keepdims=True)
    byte = np.maximum(np.where(amax > 0, np.frexp(amax)[1] - 1 + 127, 0) - down, 1)
    scale = np.exp2(byte - 127.0)
    codes = (blocks / scale).astype(np.float32).astype(dtype).astype(np.float64)
    return np.moveaxis((codes * scale).reshape(v.shape), -1, axis)


WIDE = False


def mx_kscale(k):
    if not WIDE:
        return np.ones(k)
    levels = np.array([10, -10, 5, -5, 0])
    if k % 512:
        return np.exp2(np.random.permutation(np.resize(levels, k // 32))).repeat(32)
    a = np.empty((k // 512, 16))
    for p in range(k // 512):
        a[p, :8] = np.random.permutation(np.resize(levels, 8))
        for g in range(8):
            far = levels[np.abs(levels - a[p, g]) >= 10]
            a[p, g + 8] = far[np.random.randint(len(far))]
    return np.exp2(a.ravel()).repeat(32)


def f64(x):
    return np.asarray(x).astype(np.float64)


def striped(idx):
    return np.tile(idx.reshape(-1, 16).T, (8, 1)).astype(np.uint16)


def unstriped(offs):
    return offs[:16].T.reshape(-1).astype(np.int64)


def pack_weight(w):
    k, n = w.shape
    w = f64(np.asarray(w, np.float32).astype(ml_dtypes.bfloat16)).reshape(k // 32, 32, n)
    amax = np.abs(w).max(1)
    byte = np.clip(np.where(amax > 0, np.frexp(amax)[1] - 1 + 127 - 7, 1), 1, 254)
    scaled = (w * np.exp2(127.0 - byte)[:, None, :]).reshape(k, n).astype(np.float32)
    words = np.ascontiguousarray(scaled.reshape(k // 512, 128, 4, n).transpose(0, 1, 3, 2)).astype(ml_dtypes.float8_e4m3fn).view(np.uint8)
    return words, np.ascontiguousarray(byte.astype(np.uint8).reshape(k // 512, 16, n))


def unpack_weight(words, scales):
    g, p, n, _ = words.shape
    vals = np.ascontiguousarray(words).view(ml_dtypes.float8_e4m3fn).astype(np.float64) * np.repeat(np.exp2(scales.astype(np.float64) - 127.0), 8, axis=1)[..., None]
    return vals.transpose(0, 1, 3, 2).reshape(g * 512, n)


def relu(v):
    return np.maximum(v, 0.0)


K, T, S, V, H, N = 512, 4096, 1536, 512, 512, 256


def setup_inputs():
    n = np.random.standard_normal
    s = mx_kscale(K)[:, None]
    u = mx_kscale(H)
    packed_xT = pack_weight(n((K, T)) * s)
    return {
        "x_words": packed_xT[0],
        "x_scales": packed_xT[1],
        "w1": (n((K, H)) / np.sqrt(K) / s * u).astype(np.float32),
        "w2": (n((K, H)) / np.sqrt(K) / s).astype(np.float32),
        "w3": (n((K, H)) / np.sqrt(K) / s).astype(np.float32),
        "w4": (n((H, N)) / np.sqrt(H) / u[:, None]).astype(np.float32),
        "offs": striped(np.random.permutation(T)[:S]),
    }


def reference(x_words, x_scales, w1, w2, w3, w4, offs):
    xq = unpack_weight(x_words, x_scales)[:, unstriped(offs)]
    z = (((mxq(f64(w1), 0, "e4m3").T @ xq[:, :V])) * ((mxq(f64(w2), 0, "e4m3").T @ xq[:, V:2 * V]))) * ((mxq(f64(w3), 0, "e4m3").T @ xq[:, 2 * V:3 * V]))
    return relu(mxq(f64(w4), 0, "e4m3").T @ mxq(z, 0, "e4m3"))

@@ -1,0 +1,160 @@
+from contextlib import ExitStack
+
+import concourse.mybir as mybir
+
+K, T, S, V, H, N = 512, 4096, 1536, 512, 512, 256
+FLOPS = 2 * K * H * S + 2 * H * N * V
+
+F32 = mybir.dt.float32
+BF16 = mybir.dt.bfloat16
+I32 = mybir.dt.int32
+U32 = mybir.dt.uint32
+U16 = mybir.dt.uint16
+U8 = mybir.dt.uint8
+FP8X4 = mybir.dt.float8_e4m3fn_x4
+MULT = mybir.AluOpType.mult
+RELU = mybir.ActivationFunctionType.Relu
+
+P = 128
+PACK = 4
+PIECES = 3
+VB = 128
+BLOCKS = V // VB
+HALF = H // 2
+
+
+def tile_picked_trilin_relu_p_kernel(tc, x_words, x_scales, w1, w2, w3, w4, offs, out):
+    nc = tc.nc
+    with ExitStack() as ctx:
+        keep = ctx.enter_context(tc.tile_pool(name="keep", bufs=1))
+        psum = ctx.enter_context(tc.psum_pool(name="psum", bufs=1))
+
+        offsets = keep.tile([P, S // 16], U16, name="offsets")
+        table_words = keep.tile([P, T], I32, name="table_words", align_bytes=64)
+        table_scales = keep.tile([P, T], U8, name="table_scales", tag="scales_then_words", align_bytes=64)
+
+        nc.vector.memset(table_scales[:].bitcast(I32), 0)
+        nc.sync.dma_start(offsets[:], offs)
+        raw = {}
+
+        def load_half(d, h):
+            raw[d, h] = keep.tile([P, PACK, HALF], F32, name="raw_%d_%d" % (d, h))
+            nc.sync.dma_start(out=raw[d, h][:], in_=(w1, w2, w3)[d][:, h * HALF : (h + 1) * HALF].rearrange("(p j) c -> p j c", j=PACK))
+
+        load_half(0, 0)
+        for q in range(4):
+            nc.sync.dma_start(out=table_scales[32 * q : 32 * q + 4, :].bitcast(I32), in_=x_scales[0, 4 * q : 4 * q + 4, :].bitcast(I32))
+        nc.sync.dma_start(out=table_words[:], in_=x_words[0].rearrange("p c r -> p (c r)").bitcast(I32))
+        for d, h in ((0, 1), (1, 0), (1, 1), (2, 0), (2, 1)):
+            load_half(d, h)
+        raw4 = keep.tile([P, PACK, N], F32, name="raw4")
+        w4_rows = w4.rearrange("(u t i) n -> t u i n", t=PACK, i=4)
+        for t in range(PACK):
+            nc.sync.dma_start(out=raw4[:, t, :], in_=w4_rows[t])
+
+        picked_scales = keep.tile([P, S], U8, name="picked_scales", align_bytes=64)
+        nc.vector.tensor_copy(picked_scales[:], table_scales[:].indirect(offsets[:]))
+        picked_words = {}
+
+        def gather(d, into):
+            nc.vector.tensor_copy(into, table_words[:].bitcast(U32).indirect(offsets[:, d * V // 16 : (d + 1) * V // 16]))
+            picked_words[d] = into
+
+        two = keep.tile([P, 2 * V], U32, name="picked_words_01", tag="scales_then_words", align_bytes=64)
+
+        grouped = [keep.tile([P, PACK, P * PACK], BF16, name="grouped_%d" % d, tag="grouped_%d" % d, align_bytes=64) for d in range(PIECES)]
+        codes = [keep.tile([P, H], U32, name="codes_%d" % d, align_bytes=64) for d in range(PIECES)]
+        scales = [keep.tile([P, H], U8, name="scales_%d" % d, align_bytes=64) for d in range(PIECES)]
+
+        def cast(copy, d, h):
+            copy(
+                out=grouped[d][:, :, h * HALF : (h + 1) * HALF].rearrange("p t (u i j) -> p u t j i", i=4, j=PACK),
+                in_=raw[d, h][:].rearrange("p j (u t i) -> p u t j i", t=PACK, i=4),
+            )
+
+        def quantize(d):
+            nc.vector.quantize_mx(out=codes[d][:].bitcast(FP8X4), scales=scales[d][:], in_=grouped[d][:].rearrange("p t c -> p (t c)"))
+
+        def quantize_half(d, h):
+            for t in range(PACK):
+                cols = slice(t * P + h * P // 2, t * P + (h + 1) * P // 2)
+                nc.vector.quantize_mx(out=codes[d][:, cols].bitcast(FP8X4), scales=scales[d][:, cols], in_=grouped[d][:, t, h * HALF : (h + 1) * HALF])
+
+        def product(d, b, tag):
+            bank = psum.tile([P, PACK, VB], F32, name="bank_%d_%d" % (d, b), tag=tag, bufs=4)
+            for t in range(PACK):
+                nc.tensor.matmul_mx(
+                    out=bank[:, t, :],
+                    lhsT=codes[d][:, t * P : (t + 1) * P].bitcast(FP8X4),
+                    lhsT_scale=scales[d][:, t * P : (t + 1) * P],
+                    rhs=picked_words[d][:, b * VB : (b + 1) * VB].bitcast(FP8X4),
+                    rhs_scale=picked_scales[:, d * V + b * VB : d * V + (b + 1) * VB],
+                    start=True,
+                    stop=True,
+                )
+            return bank[:].rearrange("p t v -> p v t")
+
+        cast(nc.scalar.copy, 0, 0)
+        quantize_half(0, 0)
+        gather(0, two[:, 0:V])
+        gather(1, two[:, V : 2 * V])
+        cast(nc.scalar.copy, 0, 1)
+        quantize_half(0, 1)
+        cast(nc.scalar.copy, 1, 0)
+        cast(nc.vector.tensor_copy, 1, 1)
+        quantize(1)
+        third = keep.tile([P, V], U32, name="picked_words_2", tag="grouped_1", align_bytes=64)
+        gather(2, third[:])
+        first = []
+        for b in range(BLOCKS):
+            a = keep.tile([P, VB, PACK], F32, name="first_%d" % b)
+            nc.scalar.copy(out=a[:], in_=product(0, b, "odd"))
+            first.append(a)
+        cast(nc.scalar.copy, 2, 0)
+        cast(nc.scalar.copy, 2, 1)
+        pair = []
+        for b in range(BLOCKS):
+            ab = keep.tile([P, VB, PACK], F32, name="pair_%d" % b)
+            nc.vector.tensor_tensor(ab[:], product(1, b, "even"), first[b][:], MULT)
+            pair.append(ab)
+            if b in (1, 2):
+                quantize_half(2, b - 1)
+
+        grouped4 = keep.tile([P, N, PACK], BF16, name="grouped4", align_bytes=64)
+        codes4 = keep.tile([P, N], U32, name="codes4", align_bytes=64)
+        scales4 = keep.tile([P, N], U8, name="scales4", align_bytes=64)
+        nc.scalar.copy(
+            out=grouped4[:].rearrange("p (c i) t -> p c t i", i=4),
+            in_=raw4[:].rearrange("p t (c i) -> p c t i", i=4),
+        )
+
+        z = [keep.tile([P, VB, PACK], BF16, name="z_%d" % b, align_bytes=64) for b in range(BLOCKS)]
+
+        def triple(b):
+            nc.vector.tensor_tensor(z[b][:], product(2, b, "odd"), pair[b][:], MULT)
+
+        def finish(b):
+            z_codes = keep.tile([P, VB], U32, name="z_codes_%d" % b, align_bytes=64)
+            z_scales = keep.tile([P, VB], U8, name="z_scales_%d" % b, align_bytes=64)
+            nc.vector.quantize_mx(out=z_codes[:].bitcast(FP8X4), scales=z_scales[:], in_=z[b][:].rearrange("p v t -> p (v t)"))
+            bank = psum.tile([P, PACK, VB], F32, name="out_bank_%d" % b, tag="even", bufs=4)
+            for m in range(N // P):
+                nc.tensor.matmul_mx(
+                    out=bank[:, m, :],
+                    lhsT=codes4[:, m * P : (m + 1) * P].bitcast(FP8X4),
+                    lhsT_scale=scales4[:, m * P : (m + 1) * P],
+                    rhs=z_codes[:].bitcast(FP8X4),
+                    rhs_scale=z_scales[:],
+                    start=True,
+                    stop=True,
+                )
+            result = keep.tile([P, N // P, VB], F32, name="result_%d" % b)
+            nc.scalar.activation(result[:], bank[:, 0 : N // P, :], RELU)
+            nc.sync.dma_start(out=out[:, b * VB : (b + 1) * VB].rearrange("(m p) v -> p m v", p=P), in_=result[:])
+
+        triple(0)
+        nc.vector.quantize_mx(out=codes4[:].bitcast(FP8X4), scales=scales4[:], in_=grouped4[:].rearrange("p n t -> p (n t)"))
+        for b in range(1, BLOCKS):
+            triple(b)
+            finish(b - 1)
+        finish(BLOCKS - 1)

@@ -38,22 +38,27 @@ def tile_picked_trilin_relu_p_kernel(tc, x_words, x_scales, w1, w2, w3, w4, offs
         raw = {}
 
         def load_half(d, h):
-            raw[d, h] = keep.tile([P, PACK, HALF], F32, name="raw_%d_%d" % (d, h))
+            raw[d, h] = keep.tile([P, PACK, HALF], F32, name="raw_%d_%d" % (d, h), tag="raw_%d_%d" % (d, h))
             nc.sync.dma_start(out=raw[d, h][:], in_=(w1, w2, w3)[d][:, h * HALF : (h + 1) * HALF].rearrange("(p j) c -> p j c", j=PACK))
 
         load_half(0, 0)
-        for q in range(4):
-            nc.sync.dma_start(out=table_scales[32 * q : 32 * q + 4, :].bitcast(I32), in_=x_scales[0, 4 * q : 4 * q + 4, :].bitcast(I32))
+        nc.sync.dma_start(out=table_scales[0:P:8, :].bitcast(I32), in_=x_scales[0].bitcast(I32))
+        load_half(0, 1)
         nc.sync.dma_start(out=table_words[:], in_=x_words[0].rearrange("p c r -> p (c r)").bitcast(I32))
-        for d, h in ((0, 1), (1, 0), (1, 1), (2, 0), (2, 1)):
+        spread_scales = keep.tile([P, S], U8, name="spread_scales", align_bytes=64)
+        picked_scales = keep.tile([P, S], U8, name="picked_scales", align_bytes=64)
+        nc.vector.memset(picked_scales[:].bitcast(I32), 0)
+        nc.vector.tensor_copy(spread_scales[:], table_scales[:].indirect(offsets[:]))
+        load_half(1, 0)
+        for r in range(4):
+            nc.sync.dma_start(out=picked_scales[r:P:32, :].bitcast(I32), in_=spread_scales[8 * r : P : 32, :].bitcast(I32))
+        for d, h in ((1, 1), (2, 0), (2, 1)):
             load_half(d, h)
         raw4 = keep.tile([P, PACK, N], F32, name="raw4")
         w4_rows = w4.rearrange("(u t i) n -> t u i n", t=PACK, i=4)
         for t in range(PACK):
             nc.sync.dma_start(out=raw4[:, t, :], in_=w4_rows[t])
 
-        picked_scales = keep.tile([P, S], U8, name="picked_scales", align_bytes=64)
-        nc.vector.tensor_copy(picked_scales[:], table_scales[:].indirect(offsets[:]))
         picked_words = {}
 
         def gather(d, into):
@@ -75,11 +80,6 @@ def tile_picked_trilin_relu_p_kernel(tc, x_words, x_scales, w1, w2, w3, w4, offs
         def quantize(d):
             nc.vector.quantize_mx(out=codes[d][:].bitcast(FP8X4), scales=scales[d][:], in_=grouped[d][:].rearrange("p t c -> p (t c)"))
 
-        def quantize_half(d, h):
-            for t in range(PACK):
-                cols = slice(t * P + h * P // 2, t * P + (h + 1) * P // 2)
-                nc.vector.quantize_mx(out=codes[d][:, cols].bitcast(FP8X4), scales=scales[d][:, cols], in_=grouped[d][:, t, h * HALF : (h + 1) * HALF])
-
         def product(d, b, tag):
             bank = psum.tile([P, PACK, VB], F32, name="bank_%d_%d" % (d, b), tag=tag, bufs=4)
             for t in range(PACK):
@@ -95,30 +95,26 @@ def tile_picked_trilin_relu_p_kernel(tc, x_words, x_scales, w1, w2, w3, w4, offs
             return bank[:].rearrange("p t v -> p v t")
 
         cast(nc.scalar.copy, 0, 0)
-        quantize_half(0, 0)
+        cast(nc.scalar.copy, 0, 1)
+        quantize(0)
         gather(0, two[:, 0:V])
         gather(1, two[:, V : 2 * V])
-        cast(nc.scalar.copy, 0, 1)
-        quantize_half(0, 1)
         cast(nc.scalar.copy, 1, 0)
         cast(nc.vector.tensor_copy, 1, 1)
         quantize(1)
         third = keep.tile([P, V], U32, name="picked_words_2", tag="grouped_1", align_bytes=64)
         gather(2, third[:])
-        first = []
+        first = keep.tile([P, BLOCKS, VB, PACK], F32, name="first", tag="raw_1_0")
         for b in range(BLOCKS):
-            a = keep.tile([P, VB, PACK], F32, name="first_%d" % b)
-            nc.scalar.copy(out=a[:], in_=product(0, b, "odd"))
-            first.append(a)
+            nc.scalar.copy(out=first[:, b], in_=product(0, b, "odd"))
         cast(nc.scalar.copy, 2, 0)
         cast(nc.scalar.copy, 2, 1)
         pair = []
         for b in range(BLOCKS):
             ab = keep.tile([P, VB, PACK], F32, name="pair_%d" % b)
-            nc.vector.tensor_tensor(ab[:], product(1, b, "even"), first[b][:], MULT)
+            nc.vector.tensor_tensor(ab[:], product(1, b, "even"), first[:, b], MULT)
             pair.append(ab)
-            if b in (1, 2):
-                quantize_half(2, b - 1)
+        quantize(2)
 
         grouped4 = keep.tile([P, N, PACK], BF16, name="grouped4", align_bytes=64)
         codes4 = keep.tile([P, N], U32, name="codes4", align_bytes=64)

@@ -104,17 +104,21 @@ def tile_picked_trilin_relu_p_kernel(tc, x_words, x_scales, w1, w2, w3, w4, offs
         quantize(1)
         third = keep.tile([P, V], U32, name="picked_words_2", tag="grouped_1", align_bytes=64)
         gather(2, third[:])
-        first = keep.tile([P, BLOCKS, VB, PACK], F32, name="first", tag="raw_1_0")
-        for b in range(BLOCKS):
-            nc.scalar.copy(out=first[:, b], in_=product(0, b, "odd"))
+        last = BLOCKS - 1
+        early = keep.tile([P, last, VB, PACK], F32, name="first_early", tag="raw_1_0")
+        first = [early[:, b] for b in range(last)]
+        for b in range(last):
+            nc.scalar.copy(out=first[b], in_=product(0, b, "odd"))
         cast(nc.scalar.copy, 2, 0)
         cast(nc.scalar.copy, 2, 1)
-        pair = []
-        for b in range(BLOCKS):
-            ab = keep.tile([P, VB, PACK], F32, name="pair_%d" % b)
-            nc.vector.tensor_tensor(ab[:], product(1, b, "even"), first[:, b], MULT)
-            pair.append(ab)
+        pair = keep.tile([P, BLOCKS, VB, PACK], F32, name="pair")
+        second = [product(1, b, "even") for b in range(BLOCKS)]
+        for b in range(last):
+            nc.vector.tensor_tensor(pair[:, b], second[b], first[b], MULT)
+        late = keep.tile([P, VB, PACK], F32, name="first_late", tag="raw_2_1")
+        nc.scalar.copy(out=late[:], in_=product(0, last, "even"))
         quantize(2)
+        nc.vector.tensor_tensor(pair[:, last], second[last], late[:], MULT)
 
         grouped4 = keep.tile([P, N, PACK], BF16, name="grouped4", align_bytes=64)
         codes4 = keep.tile([P, N], U32, name="codes4", align_bytes=64)
@@ -127,16 +131,16 @@ def tile_picked_trilin_relu_p_kernel(tc, x_words, x_scales, w1, w2, w3, w4, offs
         z = [keep.tile([P, VB, PACK], BF16, name="z_%d" % b, align_bytes=64) for b in range(BLOCKS)]
 
         def triple(b):
-            nc.vector.tensor_tensor(z[b][:], product(2, b, "odd"), pair[b][:], MULT)
+            nc.vector.tensor_tensor(z[b][:], product(2, b, "odd"), pair[:, b], MULT)
 
         def finish(b):
             z_codes = keep.tile([P, VB], U32, name="z_codes_%d" % b, align_bytes=64)
             z_scales = keep.tile([P, VB], U8, name="z_scales_%d" % b, align_bytes=64)
             nc.vector.quantize_mx(out=z_codes[:].bitcast(FP8X4), scales=z_scales[:], in_=z[b][:].rearrange("p v t -> p (v t)"))
-            bank = psum.tile([P, PACK, VB], F32, name="out_bank_%d" % b, tag="even", bufs=4)
-            for m in range(N // P):
+
+            def output_rows(into, m):
                 nc.tensor.matmul_mx(
-                    out=bank[:, m, :],
+                    out=into,
                     lhsT=codes4[:, m * P : (m + 1) * P].bitcast(FP8X4),
                     lhsT_scale=scales4[:, m * P : (m + 1) * P],
                     rhs=z_codes[:].bitcast(FP8X4),
@@ -144,9 +148,26 @@ def tile_picked_trilin_relu_p_kernel(tc, x_words, x_scales, w1, w2, w3, w4, offs
                     start=True,
                     stop=True,
                 )
-            result = keep.tile([P, N // P, VB], F32, name="result_%d" % b)
-            nc.scalar.activation(result[:], bank[:, 0 : N // P, :], RELU)
-            nc.sync.dma_start(out=out[:, b * VB : (b + 1) * VB].rearrange("(m p) v -> p m v", p=P), in_=result[:])
+
+            cols = slice(b * VB, (b + 1) * VB)
+            if b < last:
+                bank = psum.tile([P, PACK, VB], F32, name="out_bank_%d" % b, tag="even", bufs=4)
+                for m in range(N // P):
+                    output_rows(bank[:, m, :], m)
+                result = keep.tile([P, N // P, VB], F32, name="result_%d" % b)
+                nc.scalar.activation(result[:], bank[:, 0 : N // P, :], RELU)
+                nc.sync.dma_start(out=out[:, cols].rearrange("(m p) v -> p m v", p=P), in_=result[:])
+            else:
+                upper = psum.tile([P, PACK, VB], F32, name="out_bank_upper", tag="even", bufs=4)
+                lower = psum.tile([P, PACK, VB], F32, name="out_bank_lower", tag="odd", bufs=4)
+                output_rows(upper[:, 0, :], 0)
+                output_rows(lower[:, 0, :], 1)
+                result_upper = keep.tile([P, VB], F32, name="result_upper")
+                result_lower = keep.tile([P, VB], F32, name="result_lower")
+                nc.scalar.activation(result_upper[:], upper[:, 0, :], RELU)
+                nc.scalar.dma_start(out=out[0:P, cols], in_=result_upper[:])
+                nc.vector.tensor_scalar_max(result_lower[:], lower[:, 0, :], 0.0)
+                nc.sync.dma_start(out=out[P : 2 * P, cols], in_=result_lower[:])
 
         triple(0)
         nc.vector.quantize_mx(out=codes4[:].bitcast(FP8X4), scales=scales4[:], in_=grouped4[:].rearrange("p n t -> p (n t)"))

@@ -17,10 +17,15 @@ RELU = mybir.ActivationFunctionType.Relu
 
 P = 128
 PACK = 4
+RUN = 4
 PIECES = 3
+LIST_ROWS = 16
+QUADRANT = 32
+SPREAD = P // (K // 32)
 VB = 128
 BLOCKS = V // VB
 HALF = H // 2
+BANKS = 4
 
 
 def tile_picked_trilin_relu_p_kernel(tc, x_words, x_scales, w1, w2, w3, w4, offs, out):
@@ -29,7 +34,7 @@ def tile_picked_trilin_relu_p_kernel(tc, x_words, x_scales, w1, w2, w3, w4, offs
         keep = ctx.enter_context(tc.tile_pool(name="keep", bufs=1))
         psum = ctx.enter_context(tc.psum_pool(name="psum", bufs=1))
 
-        offsets = keep.tile([P, S // 16], U16, name="offsets")
+        offsets = keep.tile([P, S // LIST_ROWS], U16, name="offsets")
         table_words = keep.tile([P, T], I32, name="table_words", align_bytes=64)
         table_scales = keep.tile([P, T], U8, name="table_scales", tag="scales_then_words", align_bytes=64)
 
@@ -41,47 +46,54 @@ def tile_picked_trilin_relu_p_kernel(tc, x_words, x_scales, w1, w2, w3, w4, offs
             raw[d, h] = keep.tile([P, PACK, HALF], F32, name="raw_%d_%d" % (d, h), tag="raw_%d_%d" % (d, h))
             nc.sync.dma_start(out=raw[d, h][:], in_=(w1, w2, w3)[d][:, h * HALF : (h + 1) * HALF].rearrange("(p j) c -> p j c", j=PACK))
 
-        load_half(0, 0)
-        nc.sync.dma_start(out=table_scales[0:P:8, :].bitcast(I32), in_=x_scales[0].bitcast(I32))
-        load_half(0, 1)
+        raw_w1 = keep.tile([P, PACK, H], F32, name="raw_w1")
+        w1_rows = w1.rearrange("(p j) c -> p j c", j=PACK)
+        nc.sync.dma_start(out=raw_w1[:, 0 : PACK // 2, :], in_=w1_rows[:, 0 : PACK // 2, :])
+        nc.sync.dma_start(out=table_scales[0:P:SPREAD, :].bitcast(I32), in_=x_scales[0].bitcast(I32))
+        nc.sync.dma_start(out=raw_w1[:, PACK // 2 : PACK, :], in_=w1_rows[:, PACK // 2 : PACK, :])
         nc.sync.dma_start(out=table_words[:], in_=x_words[0].rearrange("p c r -> p (c r)").bitcast(I32))
+
         spread_scales = keep.tile([P, S], U8, name="spread_scales", align_bytes=64)
         picked_scales = keep.tile([P, S], U8, name="picked_scales", align_bytes=64)
         nc.vector.memset(picked_scales[:].bitcast(I32), 0)
         nc.vector.tensor_copy(spread_scales[:], table_scales[:].indirect(offsets[:]))
         load_half(1, 0)
-        for r in range(4):
-            nc.sync.dma_start(out=picked_scales[r:P:32, :].bitcast(I32), in_=spread_scales[8 * r : P : 32, :].bitcast(I32))
+        for r in range(QUADRANT // SPREAD):
+            nc.sync.dma_start(out=picked_scales[r:P:QUADRANT, :].bitcast(I32), in_=spread_scales[SPREAD * r : P : QUADRANT, :].bitcast(I32))
         for d, h in ((1, 1), (2, 0), (2, 1)):
             load_half(d, h)
+
         raw4 = keep.tile([P, PACK, N], F32, name="raw4")
-        w4_rows = w4.rearrange("(u t i) n -> t u i n", t=PACK, i=4)
+        w4_rows = w4.rearrange("(u t e) n -> t u e n", t=PACK, e=RUN)
         for t in range(PACK):
             nc.sync.dma_start(out=raw4[:, t, :], in_=w4_rows[t])
 
         picked_words = {}
 
         def gather(d, into):
-            nc.vector.tensor_copy(into, table_words[:].bitcast(U32).indirect(offsets[:, d * V // 16 : (d + 1) * V // 16]))
+            nc.vector.tensor_copy(into, table_words[:].bitcast(U32).indirect(offsets[:, d * V // LIST_ROWS : (d + 1) * V // LIST_ROWS]))
             picked_words[d] = into
 
-        two = keep.tile([P, 2 * V], U32, name="picked_words_01", tag="scales_then_words", align_bytes=64)
+        words_01 = keep.tile([P, 2 * V], U32, name="picked_words_01", tag="scales_then_words", align_bytes=64)
 
         grouped = [keep.tile([P, PACK, P * PACK], BF16, name="grouped_%d" % d, tag="grouped_%d" % d, align_bytes=64) for d in range(PIECES)]
         codes = [keep.tile([P, H], U32, name="codes_%d" % d, align_bytes=64) for d in range(PIECES)]
         scales = [keep.tile([P, H], U8, name="scales_%d" % d, align_bytes=64) for d in range(PIECES)]
 
-        def cast(copy, d, h):
+        def round_and_group(copy, into, rows):
             copy(
-                out=grouped[d][:, :, h * HALF : (h + 1) * HALF].rearrange("p t (u i j) -> p u t j i", i=4, j=PACK),
-                in_=raw[d, h][:].rearrange("p j (u t i) -> p u t j i", t=PACK, i=4),
+                out=into.rearrange("p t (u e j) -> p u t j e", e=RUN, j=PACK),
+                in_=rows.rearrange("p j (u t e) -> p u t j e", t=PACK, e=RUN),
             )
+
+        def round_half(copy, d, h):
+            round_and_group(copy, grouped[d][:, :, h * HALF : (h + 1) * HALF], raw[d, h][:])
 
         def quantize(d):
             nc.vector.quantize_mx(out=codes[d][:].bitcast(FP8X4), scales=scales[d][:], in_=grouped[d][:].rearrange("p t c -> p (t c)"))
 
         def product(d, b, tag):
-            bank = psum.tile([P, PACK, VB], F32, name="bank_%d_%d" % (d, b), tag=tag, bufs=4)
+            bank = psum.tile([P, PACK, VB], F32, name="bank_%d_%d" % (d, b), tag=tag, bufs=BANKS)
             for t in range(PACK):
                 nc.tensor.matmul_mx(
                     out=bank[:, t, :],
@@ -94,38 +106,37 @@ def tile_picked_trilin_relu_p_kernel(tc, x_words, x_scales, w1, w2, w3, w4, offs
                 )
             return bank[:].rearrange("p t v -> p v t")
 
-        cast(nc.scalar.copy, 0, 0)
-        cast(nc.scalar.copy, 0, 1)
+        round_and_group(nc.scalar.copy, grouped[0][:], raw_w1[:])
         quantize(0)
-        gather(0, two[:, 0:V])
-        gather(1, two[:, V : 2 * V])
-        cast(nc.scalar.copy, 1, 0)
-        cast(nc.vector.tensor_copy, 1, 1)
+        gather(0, words_01[:, 0:V])
+        gather(1, words_01[:, V : 2 * V])
+        round_half(nc.scalar.copy, 1, 0)
+        round_half(nc.vector.tensor_copy, 1, 1)
         quantize(1)
-        third = keep.tile([P, V], U32, name="picked_words_2", tag="grouped_1", align_bytes=64)
-        gather(2, third[:])
+        words_2 = keep.tile([P, V], U32, name="picked_words_2", tag="grouped_1", align_bytes=64)
+        gather(2, words_2[:])
+
         last = BLOCKS - 1
-        early = keep.tile([P, last, VB, PACK], F32, name="first_early", tag="raw_1_0")
-        first = [early[:, b] for b in range(last)]
+        first_early = keep.tile([P, last, VB, PACK], F32, name="first_early", tag="raw_1_0")
         for b in range(last):
-            nc.scalar.copy(out=first[b], in_=product(0, b, "odd"))
-        cast(nc.scalar.copy, 2, 0)
-        cast(nc.scalar.copy, 2, 1)
+            nc.scalar.copy(out=first_early[:, b], in_=product(0, b, "odd"))
+        round_half(nc.scalar.copy, 2, 0)
+        round_half(nc.scalar.copy, 2, 1)
         pair = keep.tile([P, BLOCKS, VB, PACK], F32, name="pair")
         second = [product(1, b, "even") for b in range(BLOCKS)]
         for b in range(last):
-            nc.vector.tensor_tensor(pair[:, b], second[b], first[b], MULT)
-        late = keep.tile([P, VB, PACK], F32, name="first_late", tag="raw_2_1")
-        nc.scalar.copy(out=late[:], in_=product(0, last, "even"))
+            nc.vector.tensor_tensor(pair[:, b], second[b], first_early[:, b], MULT)
+        first_late = keep.tile([P, VB, PACK], F32, name="first_late", tag="raw_2_1")
+        nc.scalar.copy(out=first_late[:], in_=product(0, last, "even"))
         quantize(2)
-        nc.vector.tensor_tensor(pair[:, last], second[last], late[:], MULT)
+        nc.vector.tensor_tensor(pair[:, last], second[last], first_late[:], MULT)
 
         grouped4 = keep.tile([P, N, PACK], BF16, name="grouped4", align_bytes=64)
         codes4 = keep.tile([P, N], U32, name="codes4", align_bytes=64)
         scales4 = keep.tile([P, N], U8, name="scales4", align_bytes=64)
         nc.scalar.copy(
-            out=grouped4[:].rearrange("p (c i) t -> p c t i", i=4),
-            in_=raw4[:].rearrange("p t (c i) -> p c t i", i=4),
+            out=grouped4[:].rearrange("p (c e) t -> p c t e", e=RUN),
+            in_=raw4[:].rearrange("p t (c e) -> p c t e", e=RUN),
         )
 
         z = [keep.tile([P, VB, PACK], BF16, name="z_%d" % b, align_bytes=64) for b in range(BLOCKS)]
@@ -151,15 +162,15 @@ def tile_picked_trilin_relu_p_kernel(tc, x_words, x_scales, w1, w2, w3, w4, offs
 
             cols = slice(b * VB, (b + 1) * VB)
             if b < last:
-                bank = psum.tile([P, PACK, VB], F32, name="out_bank_%d" % b, tag="even", bufs=4)
+                bank = psum.tile([P, PACK, VB], F32, name="out_bank_%d" % b, tag="even", bufs=BANKS)
                 for m in range(N // P):
                     output_rows(bank[:, m, :], m)
                 result = keep.tile([P, N // P, VB], F32, name="result_%d" % b)
                 nc.scalar.activation(result[:], bank[:, 0 : N // P, :], RELU)
                 nc.sync.dma_start(out=out[:, cols].rearrange("(m p) v -> p m v", p=P), in_=result[:])
             else:
-                upper = psum.tile([P, PACK, VB], F32, name="out_bank_upper", tag="even", bufs=4)
-                lower = psum.tile([P, PACK, VB], F32, name="out_bank_lower", tag="odd", bufs=4)
+                upper = psum.tile([P, PACK, VB], F32, name="out_bank_upper", tag="even", bufs=BANKS)
+                lower = psum.tile([P, PACK, VB], F32, name="out_bank_lower", tag="odd", bufs=BANKS)
                 output_rows(upper[:, 0, :], 0)
                 output_rows(lower[:, 0, :], 1)
                 result_upper = keep.tile([P, VB], F32, name="result_upper")
@@ -174,4 +185,4 @@ def tile_picked_trilin_relu_p_kernel(tc, x_words, x_scales, w1, w2, w3, w4, offs
         for b in range(1, BLOCKS):
             triple(b)
             finish(b - 1)
-        finish(BLOCKS - 1)
+        finish(last)

@@ -38,6 +38,11 @@ def tile_picked_trilin_relu_p_kernel(tc, x_words, x_scales, w1, w2, w3, w4, offs
         table_words = keep.tile([P, T], I32, name="table_words", align_bytes=64)
         table_scales = keep.tile([P, T], U8, name="table_scales", tag="scales_then_words", align_bytes=64)
 
+        warm_in = keep.tile([P, 1], F32, name="warm_in")
+        warm_out = keep.tile([P, 1], F32, name="warm_out")
+        nc.gpsimd.memset(warm_in[:], 0.0)
+        nc.scalar.activation(warm_out[:], warm_in[:], RELU)
+
         nc.vector.memset(table_scales[:].bitcast(I32), 0)
         nc.sync.dma_start(offsets[:], offs)
         raw = {}
@@ -60,8 +65,9 @@ def tile_picked_trilin_relu_p_kernel(tc, x_words, x_scales, w1, w2, w3, w4, offs
         load_half(1, 0)
         for r in range(QUADRANT // SPREAD):
             nc.sync.dma_start(out=picked_scales[r:P:QUADRANT, :].bitcast(I32), in_=spread_scales[SPREAD * r : P : QUADRANT, :].bitcast(I32))
-        for d, h in ((1, 1), (2, 0), (2, 1)):
-            load_half(d, h)
+        load_half(1, 1)
+        raw_w3 = keep.tile([P, PACK, H], F32, name="raw_w3", tag="raw_w3")
+        nc.sync.dma_start(out=raw_w3[:], in_=w3.rearrange("(p j) c -> p j c", j=PACK))
 
         raw4 = keep.tile([P, PACK, N], F32, name="raw4")
         w4_rows = w4.rearrange("(u t e) n -> t u e n", t=PACK, e=RUN)
@@ -120,13 +126,12 @@ def tile_picked_trilin_relu_p_kernel(tc, x_words, x_scales, w1, w2, w3, w4, offs
         first_early = keep.tile([P, last, VB, PACK], F32, name="first_early", tag="raw_1_0")
         for b in range(last):
             nc.scalar.copy(out=first_early[:, b], in_=product(0, b, "odd"))
-        round_half(nc.scalar.copy, 2, 0)
-        round_half(nc.scalar.copy, 2, 1)
+        round_and_group(nc.scalar.copy, grouped[2][:], raw_w3[:])
         pair = keep.tile([P, BLOCKS, VB, PACK], F32, name="pair")
         second = [product(1, b, "even") for b in range(BLOCKS)]
         for b in range(last):
             nc.vector.tensor_tensor(pair[:, b], second[b], first_early[:, b], MULT)
-        first_late = keep.tile([P, VB, PACK], F32, name="first_late", tag="raw_2_1")
+        first_late = keep.tile([P, VB, PACK], F32, name="first_late", tag="raw_w3")
         nc.scalar.copy(out=first_late[:], in_=product(0, last, "even"))
         quantize(2)
         nc.vector.tensor_tensor(pair[:, last], second[last], first_late[:], MULT)

@@ -32,6 +32,7 @@ def tile_picked_trilin_relu_p_kernel(tc, x_words, x_scales, w1, w2, w3, w4, offs
     nc = tc.nc
     with ExitStack() as ctx:
         keep = ctx.enter_context(tc.tile_pool(name="keep", bufs=1))
+        shared = ctx.enter_context(tc.tile_pool(name="shared", bufs=1))
         psum = ctx.enter_context(tc.psum_pool(name="psum", bufs=1))
 
         offsets = keep.tile([P, S // LIST_ROWS], U16, name="offsets")
@@ -48,7 +49,7 @@ def tile_picked_trilin_relu_p_kernel(tc, x_words, x_scales, w1, w2, w3, w4, offs
         raw = {}
 
         def load_half(d, h):
-            raw[d, h] = keep.tile([P, PACK, HALF], F32, name="raw_%d_%d" % (d, h), tag="raw_%d_%d" % (d, h))
+            raw[d, h] = shared.tile([P, PACK, HALF], F32, name="raw_%d_%d" % (d, h), offset=(16384, 0)[h], align_bytes=64)
             nc.sync.dma_start(out=raw[d, h][:], in_=(w1, w2, w3)[d][:, h * HALF : (h + 1) * HALF].rearrange("(p j) c -> p j c", j=PACK))
 
         raw_w1 = keep.tile([P, PACK, H], F32, name="raw_w1")
@@ -66,7 +67,7 @@ def tile_picked_trilin_relu_p_kernel(tc, x_words, x_scales, w1, w2, w3, w4, offs
         for r in range(QUADRANT // SPREAD):
             nc.sync.dma_start(out=picked_scales[r:P:QUADRANT, :].bitcast(I32), in_=spread_scales[SPREAD * r : P : QUADRANT, :].bitcast(I32))
         load_half(1, 1)
-        raw_w3 = keep.tile([P, PACK, H], F32, name="raw_w3", tag="raw_w3")
+        raw_w3 = shared.tile([P, PACK, H], F32, name="raw_w3", offset=8192, align_bytes=64)
         nc.sync.dma_start(out=raw_w3[:], in_=w3.rearrange("(p j) c -> p j c", j=PACK))
 
         raw4 = keep.tile([P, PACK, N], F32, name="raw4")
@@ -86,14 +87,14 @@ def tile_picked_trilin_relu_p_kernel(tc, x_words, x_scales, w1, w2, w3, w4, offs
         codes = [keep.tile([P, H], U32, name="codes_%d" % d, align_bytes=64) for d in range(PIECES)]
         scales = [keep.tile([P, H], U8, name="scales_%d" % d, align_bytes=64) for d in range(PIECES)]
 
-        def round_and_group(copy, into, rows):
+        def round_and_group(copy, into, rows, slots):
             copy(
-                out=into.rearrange("p t (u e j) -> p u t j e", e=RUN, j=PACK),
-                in_=rows.rearrange("p j (u t e) -> p u t j e", t=PACK, e=RUN),
+                out=into[:, slots].rearrange("p t (u e j) -> p u t j e", e=RUN, j=PACK),
+                in_=rows.rearrange("p j (u t e) -> p u t j e", t=PACK, e=RUN)[:, :, slots],
             )
 
-        def round_half(copy, d, h):
-            round_and_group(copy, grouped[d][:, :, h * HALF : (h + 1) * HALF], raw[d, h][:])
+        def round_half(copy, d, h, slots):
+            round_and_group(copy, grouped[d][:, :, h * HALF : (h + 1) * HALF], raw[d, h][:], slots)
 
         def quantize(d):
             nc.vector.quantize_mx(out=codes[d][:].bitcast(FP8X4), scales=scales[d][:], in_=grouped[d][:].rearrange("p t c -> p (t c)"))
@@ -112,29 +113,37 @@ def tile_picked_trilin_relu_p_kernel(tc, x_words, x_scales, w1, w2, w3, w4, offs
                 )
             return bank[:].rearrange("p t v -> p v t")
 
-        round_and_group(nc.scalar.copy, grouped[0][:], raw_w1[:])
+        every = slice(0, PACK)
+        round_and_group(nc.scalar.copy, grouped[0][:], raw_w1[:], every)
         quantize(0)
         gather(0, words_01[:, 0:V])
         gather(1, words_01[:, V : 2 * V])
-        round_half(nc.scalar.copy, 1, 0)
-        round_half(nc.vector.tensor_copy, 1, 1)
+        round_half(nc.scalar.copy, 1, 0, every)
+        round_half(nc.vector.tensor_copy, 1, 1, slice(0, 2))
+        round_half(nc.scalar.copy, 1, 1, slice(2, 4))
         quantize(1)
-        words_2 = keep.tile([P, V], U32, name="picked_words_2", tag="grouped_1", align_bytes=64)
+        words_2 = shared.tile([P, V], U32, name="picked_words_2", offset=0, align_bytes=64)
         gather(2, words_2[:])
 
         last = BLOCKS - 1
-        first_early = keep.tile([P, last, VB, PACK], F32, name="first_early", tag="raw_1_0")
+        first_early = shared.tile([P, last, VB, PACK], F32, name="first_early", offset=2048, align_bytes=64)
         for b in range(last):
             nc.scalar.copy(out=first_early[:, b], in_=product(0, b, "odd"))
-        round_and_group(nc.scalar.copy, grouped[2][:], raw_w3[:])
-        pair = keep.tile([P, BLOCKS, VB, PACK], F32, name="pair")
         second = [product(1, b, "even") for b in range(BLOCKS)]
-        for b in range(last):
-            nc.vector.tensor_tensor(pair[:, b], second[b], first_early[:, b], MULT)
-        first_late = keep.tile([P, VB, PACK], F32, name="first_late", tag="raw_w3")
-        nc.scalar.copy(out=first_late[:], in_=product(0, last, "even"))
+        pair = [keep.tile([P, VB, PACK], F32, name="pair_%d" % b) for b in range(2)]
+        for b in range(2):
+            nc.vector.tensor_tensor(pair[b][:], second[b], first_early[:, b], MULT)
+        round_and_group(nc.scalar.copy, grouped[2][:], raw_w3[:], slice(0, 3))
+        round_and_group(nc.vector.tensor_copy, grouped[2][:], raw_w3[:], slice(3, 4))
         quantize(2)
-        nc.vector.tensor_tensor(pair[:, last], second[last], first_late[:], MULT)
+        pair.append(shared.tile([P, VB, PACK], F32, name="pair_2", offset=10240, align_bytes=64))
+        nc.vector.tensor_tensor(pair[2][:], second[2], first_early[:, 2], MULT)
+        first_late = shared.tile([P, VB, PACK], F32, name="first_late", offset=8192, align_bytes=64)
+        second_late = shared.tile([P, VB, PACK], F32, name="second_late", offset=12288, align_bytes=64)
+        nc.scalar.copy(out=first_late[:], in_=product(0, last, "odd"))
+        nc.scalar.copy(out=second_late[:], in_=second[last])
+        pair.append(keep.tile([P, VB, PACK], F32, name="pair_3", tag="grouped_2", align_bytes=64))
+        nc.gpsimd.tensor_tensor(pair[last][:], second_late[:], first_late[:], MULT)
 
         grouped4 = keep.tile([P, N, PACK], BF16, name="grouped4", align_bytes=64)
         codes4 = keep.tile([P, N], U32, name="codes4", align_bytes=64)
@@ -147,7 +156,7 @@ def tile_picked_trilin_relu_p_kernel(tc, x_words, x_scales, w1, w2, w3, w4, offs
         z = [keep.tile([P, VB, PACK], BF16, name="z_%d" % b, align_bytes=64) for b in range(BLOCKS)]
 
         def triple(b):
-            nc.vector.tensor_tensor(z[b][:], product(2, b, "odd"), pair[:, b], MULT)
+            nc.vector.tensor_tensor(z[b][:], product(2, b, "odd"), pair[b][:], MULT)
 
         def finish(b):
             z_codes = keep.tile([P, VB], U32, name="z_codes_%d" % b, align_bytes=64)

@@ -17,7 +17,7 @@ RELU = mybir.ActivationFunctionType.Relu
 
 P = 128
 PACK = 4
-RUN = 4
+RUN = 2
 PIECES = 3
 LIST_ROWS = 16
 QUADRANT = 32

@@ -25,6 +25,7 @@ SPREAD = P // (K // 32)
 VB = 128
 BLOCKS = V // VB
 HALF = H // 2
+ROW0 = 4
 BANKS = 4
 
 
@@ -55,7 +56,7 @@ def tile_picked_trilin_relu_p_kernel(tc, x_words, x_scales, w1, w2, w3, w4, offs
         raw_w1 = keep.tile([P, PACK, H], F32, name="raw_w1")
         w1_rows = w1.rearrange("(p j) c -> p j c", j=PACK)
         nc.sync.dma_start(out=raw_w1[:, 0 : PACK // 2, :], in_=w1_rows[:, 0 : PACK // 2, :])
-        nc.sync.dma_start(out=table_scales[0:P:SPREAD, :].bitcast(I32), in_=x_scales[0].bitcast(I32))
+        nc.sync.dma_start(out=table_scales[ROW0:P:SPREAD, :].bitcast(I32), in_=x_scales[0].bitcast(I32))
         nc.sync.dma_start(out=raw_w1[:, PACK // 2 : PACK, :], in_=w1_rows[:, PACK // 2 : PACK, :])
         nc.sync.dma_start(out=table_words[:], in_=x_words[0].rearrange("p c r -> p (c r)").bitcast(I32))
 
@@ -65,7 +66,7 @@ def tile_picked_trilin_relu_p_kernel(tc, x_words, x_scales, w1, w2, w3, w4, offs
         nc.vector.tensor_copy(spread_scales[:], table_scales[:].indirect(offsets[:]))
         load_half(1, 0)
         for r in range(QUADRANT // SPREAD):
-            nc.sync.dma_start(out=picked_scales[r:P:QUADRANT, :].bitcast(I32), in_=spread_scales[SPREAD * r : P : QUADRANT, :].bitcast(I32))
+            nc.sync.dma_start(out=picked_scales[r:P:QUADRANT, :].bitcast(I32), in_=spread_scales[ROW0 + SPREAD * r : P : QUADRANT, :].bitcast(I32))
         load_half(1, 1)
         raw_w3 = shared.tile([P, PACK, H], F32, name="raw_w3", offset=8192, align_bytes=64)
         nc.sync.dma_start(out=raw_w3[:], in_=w3.rearrange("(p j) c -> p j c", j=PACK))
@@ -96,11 +97,12 @@ def tile_picked_trilin_relu_p_kernel(tc, x_words, x_scales, w1, w2, w3, w4, offs
         def round_half(copy, d, h, slots):
             round_and_group(copy, grouped[d][:, :, h * HALF : (h + 1) * HALF], raw[d, h][:], slots)
 
-        def quantize(d):
-            nc.vector.quantize_mx(out=codes[d][:].bitcast(FP8X4), scales=scales[d][:], in_=grouped[d][:].rearrange("p t c -> p (t c)"))
+        def quantize(d, t0=0, t1=PACK):
+            cols = slice(t0 * P, t1 * P)
+            nc.vector.quantize_mx(out=codes[d][:, cols].bitcast(FP8X4), scales=scales[d][:, cols], in_=grouped[d][:, t0:t1].rearrange("p t c -> p (t c)"))
 
         def product(d, b, tag):
-            bank = psum.tile([P, PACK, VB], F32, name="bank_%d_%d" % (d, b), tag=tag, bufs=BANKS)
+            bank = psum.tile([P, PACK, VB], F32, name="bank_%d_%d" % (d, b), tag="bank_%d" % tag)
             for t in range(PACK):
                 nc.tensor.matmul_mx(
                     out=bank[:, t, :],
@@ -128,20 +130,21 @@ def tile_picked_trilin_relu_p_kernel(tc, x_words, x_scales, w1, w2, w3, w4, offs
         last = BLOCKS - 1
         first_early = shared.tile([P, last, VB, PACK], F32, name="first_early", offset=2048, align_bytes=64)
         for b in range(last):
-            nc.scalar.copy(out=first_early[:, b], in_=product(0, b, "odd"))
-        second = [product(1, b, "even") for b in range(BLOCKS)]
+            nc.scalar.copy(out=first_early[:, b], in_=product(0, b, b))
+        second = [product(1, b, BLOCKS + b) for b in range(last)]
         pair = [keep.tile([P, VB, PACK], F32, name="pair_%d" % b) for b in range(2)]
         for b in range(2):
             nc.vector.tensor_tensor(pair[b][:], second[b], first_early[:, b], MULT)
         round_and_group(nc.scalar.copy, grouped[2][:], raw_w3[:], slice(0, 3))
         round_and_group(nc.vector.tensor_copy, grouped[2][:], raw_w3[:], slice(3, 4))
-        quantize(2)
+        quantize(2, 0, 2)
+        quantize(2, 2, 4)
         pair.append(shared.tile([P, VB, PACK], F32, name="pair_2", offset=10240, align_bytes=64))
         nc.vector.tensor_tensor(pair[2][:], second[2], first_early[:, 2], MULT)
         first_late = shared.tile([P, VB, PACK], F32, name="first_late", offset=8192, align_bytes=64)
         second_late = shared.tile([P, VB, PACK], F32, name="second_late", offset=12288, align_bytes=64)
-        nc.scalar.copy(out=first_late[:], in_=product(0, last, "odd"))
-        nc.scalar.copy(out=second_late[:], in_=second[last])
+        nc.scalar.copy(out=first_late[:], in_=product(0, last, BLOCKS))
+        nc.scalar.copy(out=second_late[:], in_=product(1, last, BLOCKS + 1))
         pair.append(keep.tile([P, VB, PACK], F32, name="pair_3", tag="grouped_2", align_bytes=64))
         nc.gpsimd.tensor_tensor(pair[last][:], second_late[:], first_late[:], MULT)
 
@@ -156,7 +159,7 @@ def tile_picked_trilin_relu_p_kernel(tc, x_words, x_scales, w1, w2, w3, w4, offs
         z = [keep.tile([P, VB, PACK], BF16, name="z_%d" % b, align_bytes=64) for b in range(BLOCKS)]
 
         def triple(b):
-            nc.vector.tensor_tensor(z[b][:], product(2, b, "odd"), pair[b][:], MULT)
+            nc.vector.tensor_tensor(z[b][:], product(2, b, (0, 4, 5, 6)[b]), pair[b][:], MULT)
 
         def finish(b):
             z_codes = keep.tile([P, VB], U32, name="z_codes_%d" % b, align_bytes=64)
@@ -176,15 +179,15 @@ def tile_picked_trilin_relu_p_kernel(tc, x_words, x_scales, w1, w2, w3, w4, offs
 
             cols = slice(b * VB, (b + 1) * VB)
             if b < last:
-                bank = psum.tile([P, PACK, VB], F32, name="out_bank_%d" % b, tag="even", bufs=BANKS)
+                bank = psum.tile([P, PACK, VB], F32, name="out_bank_%d" % b, tag="bank_%d" % (1, 2, 3)[b])
                 for m in range(N // P):
                     output_rows(bank[:, m, :], m)
                 result = keep.tile([P, N // P, VB], F32, name="result_%d" % b)
                 nc.scalar.activation(result[:], bank[:, 0 : N // P, :], RELU)
                 nc.sync.dma_start(out=out[:, cols].rearrange("(m p) v -> p m v", p=P), in_=result[:])
             else:
-                upper = psum.tile([P, PACK, VB], F32, name="out_bank_upper", tag="even", bufs=BANKS)
-                lower = psum.tile([P, PACK, VB], F32, name="out_bank_lower", tag="odd", bufs=BANKS)
+                upper = psum.tile([P, PACK, VB], F32, name="out_bank_upper", tag="bank_7")
+                lower = psum.tile([P, PACK, VB], F32, name="out_bank_lower", tag="bank_0")
                 output_rows(upper[:, 0, :], 0)
                 output_rows(lower[:, 0, :], 1)
                 result_upper = keep.tile([P, VB], F32, name="result_upper")
@@ -195,8 +198,9 @@ def tile_picked_trilin_relu_p_kernel(tc, x_words, x_scales, w1, w2, w3, w4, offs
                 nc.sync.dma_start(out=out[P : 2 * P, cols], in_=result_lower[:])
 
         triple(0)
+        triple(1)
         nc.vector.quantize_mx(out=codes4[:].bitcast(FP8X4), scales=scales4[:], in_=grouped4[:].rearrange("p n t -> p (n t)"))
-        for b in range(1, BLOCKS):
-            triple(b)
-            finish(b - 1)
-        finish(last)
+        for b in range(BLOCKS):
+            finish(b)
+            if b + 2 < BLOCKS:
+                triple(b + 2)

@@ -13,6 +13,7 @@ U16 = mybir.dt.uint16
 U8 = mybir.dt.uint8
 FP8X4 = mybir.dt.float8_e4m3fn_x4
 MULT = mybir.AluOpType.mult
+ADD = mybir.AluOpType.add
 RELU = mybir.ActivationFunctionType.Relu
 
 P = 128
@@ -135,8 +136,21 @@ def tile_picked_trilin_relu_p_kernel(tc, x_words, x_scales, w1, w2, w3, w4, offs
         pair = [keep.tile([P, VB, PACK], F32, name="pair_%d" % b) for b in range(2)]
         for b in range(2):
             nc.vector.tensor_tensor(pair[b][:], second[b], first_early[:, b], MULT)
-        round_and_group(nc.scalar.copy, grouped[2][:], raw_w3[:], slice(0, 3))
-        round_and_group(nc.vector.tensor_copy, grouped[2][:], raw_w3[:], slice(3, 4))
+        round_and_group(nc.scalar.copy, grouped[2][:], raw_w3[:], slice(0, 2))
+        middle = H // (PACK * RUN) // 2
+        nc.scalar.copy(
+            out=grouped[2][:, 2].rearrange("p (u e j) -> p u j e", e=RUN, j=PACK)[:, 0:middle],
+            in_=raw_w3[:].rearrange("p j (u t e) -> p t u j e", t=PACK, e=RUN)[:, 2, 0:middle],
+        )
+        for t, u0 in ((3, 0), (2, middle)):
+            nc.gpsimd.tensor_scalar(
+                grouped[2][:, t].rearrange("p (u e j) -> p u e j", e=RUN, j=PACK)[:, u0:],
+                raw_w3[:].rearrange("p j (u t e) -> p t u e j", t=PACK, e=RUN)[:, t, u0:],
+                1.0,
+                0.0,
+                MULT,
+                ADD,
+            )
         quantize(2, 0, 2)
         quantize(2, 2, 4)
         pair.append(shared.tile([P, VB, PACK], F32, name="pair_2", offset=10240, align_bytes=64))
@@ -197,10 +211,11 @@ def tile_picked_trilin_relu_p_kernel(tc, x_words, x_scales, w1, w2, w3, w4, offs
                 nc.vector.tensor_scalar_max(result_lower[:], lower[:, 0, :], 0.0)
                 nc.sync.dma_start(out=out[P : 2 * P, cols], in_=result_lower[:])
 
-        triple(0)
-        triple(1)
+        for b in range(last):
+            triple(b)
         nc.vector.quantize_mx(out=codes4[:].bitcast(FP8X4), scales=scales4[:], in_=grouped4[:].rearrange("p n t -> p (n t)"))
-        for b in range(BLOCKS):
-            finish(b)
-            if b + 2 < BLOCKS:
-                triple(b + 2)
+        finish(0)
+        finish(1)
+        triple(last)
+        finish(2)
+        finish(last)

@@ -25,9 +25,21 @@ QUADRANT = 32
 SPREAD = P // (K // 32)
 VB = 128
 BLOCKS = V // VB
+LAST = BLOCKS - 1
 HALF = H // 2
 ROW0 = 4
-BANKS = 4
+W3_SPLIT = H // (PACK * RUN) // 2
+
+BLOCK_BYTES = VB * PACK * 4
+W2_HIGH_AT = 0
+W3_AT = 4 * BLOCK_BYTES
+W2_LOW_AT = 8 * BLOCK_BYTES
+
+FIRST_BANKS = (0, 1, 2, 4)
+SECOND_BANKS = (4, 5, 6, 5)
+THIRD_BANKS = (0, 4, 5, 6)
+OUT_BANKS = (1, 2, 3)
+UPPER_BANK, LOWER_BANK = 7, 0
 
 
 def tile_picked_trilin_relu_p_kernel(tc, x_words, x_scales, w1, w2, w3, w4, offs, out):
@@ -41,18 +53,13 @@ def tile_picked_trilin_relu_p_kernel(tc, x_words, x_scales, w1, w2, w3, w4, offs
         table_words = keep.tile([P, T], I32, name="table_words", align_bytes=64)
         table_scales = keep.tile([P, T], U8, name="table_scales", tag="scales_then_words", align_bytes=64)
 
-        warm_in = keep.tile([P, 1], F32, name="warm_in")
-        warm_out = keep.tile([P, 1], F32, name="warm_out")
-        nc.gpsimd.memset(warm_in[:], 0.0)
-        nc.scalar.activation(warm_out[:], warm_in[:], RELU)
-
         nc.vector.memset(table_scales[:].bitcast(I32), 0)
         nc.sync.dma_start(offsets[:], offs)
-        raw = {}
+        raw_w2 = {}
 
-        def load_half(d, h):
-            raw[d, h] = shared.tile([P, PACK, HALF], F32, name="raw_%d_%d" % (d, h), offset=(16384, 0)[h], align_bytes=64)
-            nc.sync.dma_start(out=raw[d, h][:], in_=(w1, w2, w3)[d][:, h * HALF : (h + 1) * HALF].rearrange("(p j) c -> p j c", j=PACK))
+        def load_w2_half(h):
+            raw_w2[h] = shared.tile([P, PACK, HALF], F32, name="raw_w2_%d" % h, offset=(W2_LOW_AT, W2_HIGH_AT)[h], align_bytes=64)
+            nc.sync.dma_start(out=raw_w2[h][:], in_=w2[:, h * HALF : (h + 1) * HALF].rearrange("(p j) c -> p j c", j=PACK))
 
         raw_w1 = keep.tile([P, PACK, H], F32, name="raw_w1")
         w1_rows = w1.rearrange("(p j) c -> p j c", j=PACK)
@@ -65,11 +72,11 @@ def tile_picked_trilin_relu_p_kernel(tc, x_words, x_scales, w1, w2, w3, w4, offs
         picked_scales = keep.tile([P, S], U8, name="picked_scales", align_bytes=64)
         nc.vector.memset(picked_scales[:].bitcast(I32), 0)
         nc.vector.tensor_copy(spread_scales[:], table_scales[:].indirect(offsets[:]))
-        load_half(1, 0)
+        load_w2_half(0)
         for r in range(QUADRANT // SPREAD):
             nc.sync.dma_start(out=picked_scales[r:P:QUADRANT, :].bitcast(I32), in_=spread_scales[ROW0 + SPREAD * r : P : QUADRANT, :].bitcast(I32))
-        load_half(1, 1)
-        raw_w3 = shared.tile([P, PACK, H], F32, name="raw_w3", offset=8192, align_bytes=64)
+        load_w2_half(1)
+        raw_w3 = shared.tile([P, PACK, H], F32, name="raw_w3", offset=W3_AT, align_bytes=64)
         nc.sync.dma_start(out=raw_w3[:], in_=w3.rearrange("(p j) c -> p j c", j=PACK))
 
         raw4 = keep.tile([P, PACK, N], F32, name="raw4")
@@ -95,15 +102,15 @@ def tile_picked_trilin_relu_p_kernel(tc, x_words, x_scales, w1, w2, w3, w4, offs
                 in_=rows.rearrange("p j (u t e) -> p u t j e", t=PACK, e=RUN)[:, :, slots],
             )
 
-        def round_half(copy, d, h, slots):
-            round_and_group(copy, grouped[d][:, :, h * HALF : (h + 1) * HALF], raw[d, h][:], slots)
+        def round_w2_half(copy, h, slots):
+            round_and_group(copy, grouped[1][:, :, h * HALF : (h + 1) * HALF], raw_w2[h][:], slots)
 
         def quantize(d, t0=0, t1=PACK):
             cols = slice(t0 * P, t1 * P)
             nc.vector.quantize_mx(out=codes[d][:, cols].bitcast(FP8X4), scales=scales[d][:, cols], in_=grouped[d][:, t0:t1].rearrange("p t c -> p (t c)"))
 
-        def product(d, b, tag):
-            bank = psum.tile([P, PACK, VB], F32, name="bank_%d_%d" % (d, b), tag="bank_%d" % tag)
+        def product(d, b):
+            bank = psum.tile([P, PACK, VB], F32, name="bank_%d_%d" % (d, b), tag="bank_%d" % (FIRST_BANKS, SECOND_BANKS, THIRD_BANKS)[d][b])
             for t in range(PACK):
                 nc.tensor.matmul_mx(
                     out=bank[:, t, :],
@@ -116,51 +123,56 @@ def tile_picked_trilin_relu_p_kernel(tc, x_words, x_scales, w1, w2, w3, w4, offs
                 )
             return bank[:].rearrange("p t v -> p v t")
 
+        warm = keep.tile([P, 1], F32, name="warm")
+        nc.scalar.activation(warm[:], raw_w1[:, 0, 0:1], RELU)
+
         every = slice(0, PACK)
         round_and_group(nc.scalar.copy, grouped[0][:], raw_w1[:], every)
         quantize(0)
         gather(0, words_01[:, 0:V])
         gather(1, words_01[:, V : 2 * V])
-        round_half(nc.scalar.copy, 1, 0, every)
-        round_half(nc.vector.tensor_copy, 1, 1, slice(0, 2))
-        round_half(nc.scalar.copy, 1, 1, slice(2, 4))
-        quantize(1)
-        words_2 = shared.tile([P, V], U32, name="picked_words_2", offset=0, align_bytes=64)
-        gather(2, words_2[:])
 
-        last = BLOCKS - 1
-        first_early = shared.tile([P, last, VB, PACK], F32, name="first_early", offset=2048, align_bytes=64)
-        for b in range(last):
-            nc.scalar.copy(out=first_early[:, b], in_=product(0, b, b))
-        second = [product(1, b, BLOCKS + b) for b in range(last)]
+        round_w2_half(nc.scalar.copy, 0, every)
+        round_w2_half(nc.vector.tensor_copy, 1, slice(0, PACK // 2))
+        round_w2_half(nc.scalar.copy, 1, slice(PACK // 2, PACK))
+        quantize(1)
+
+        words_2 = shared.tile([P, V], U32, name="picked_words_2", offset=W2_HIGH_AT, align_bytes=64)
+        gather(2, words_2[:])
+        first_early = shared.tile([P, LAST, VB, PACK], F32, name="first_early", offset=W2_HIGH_AT + BLOCK_BYTES, align_bytes=64)
+        for b in range(LAST):
+            nc.scalar.copy(out=first_early[:, b], in_=product(0, b))
+        second = [product(1, b) for b in range(LAST)]
+
         pair = [keep.tile([P, VB, PACK], F32, name="pair_%d" % b) for b in range(2)]
         for b in range(2):
             nc.vector.tensor_tensor(pair[b][:], second[b], first_early[:, b], MULT)
-        round_and_group(nc.scalar.copy, grouped[2][:], raw_w3[:], slice(0, 2))
-        middle = H // (PACK * RUN) // 2
+
+        round_and_group(nc.scalar.copy, grouped[2][:], raw_w3[:], slice(0, PACK // 2))
         nc.scalar.copy(
-            out=grouped[2][:, 2].rearrange("p (u e j) -> p u j e", e=RUN, j=PACK)[:, 0:middle],
-            in_=raw_w3[:].rearrange("p j (u t e) -> p t u j e", t=PACK, e=RUN)[:, 2, 0:middle],
+            out=grouped[2][:, 2].rearrange("p (u e j) -> p u j e", e=RUN, j=PACK)[:, 0:W3_SPLIT],
+            in_=raw_w3[:].rearrange("p j (u t e) -> p t u j e", t=PACK, e=RUN)[:, 2, 0:W3_SPLIT],
         )
-        for t, u0 in ((3, 0), (2, middle)):
+        for t, u0 in ((3, 0), (2, W3_SPLIT)):
             nc.gpsimd.tensor_scalar(
-                grouped[2][:, t].rearrange("p (u e j) -> p u e j", e=RUN, j=PACK)[:, u0:],
-                raw_w3[:].rearrange("p j (u t e) -> p t u e j", t=PACK, e=RUN)[:, t, u0:],
+                grouped[2][:, t].rearrange("p (u e j) -> p u j e", e=RUN, j=PACK)[:, u0:],
+                raw_w3[:].rearrange("p j (u t e) -> p t u j e", t=PACK, e=RUN)[:, t, u0:],
                 1.0,
                 0.0,
                 MULT,
                 ADD,
             )
-        quantize(2, 0, 2)
-        quantize(2, 2, 4)
-        pair.append(shared.tile([P, VB, PACK], F32, name="pair_2", offset=10240, align_bytes=64))
+        quantize(2, 0, PACK // 2)
+        quantize(2, PACK // 2, PACK)
+
+        pair.append(shared.tile([P, VB, PACK], F32, name="pair_2", offset=W3_AT + BLOCK_BYTES, align_bytes=64))
         nc.vector.tensor_tensor(pair[2][:], second[2], first_early[:, 2], MULT)
-        first_late = shared.tile([P, VB, PACK], F32, name="first_late", offset=8192, align_bytes=64)
-        second_late = shared.tile([P, VB, PACK], F32, name="second_late", offset=12288, align_bytes=64)
-        nc.scalar.copy(out=first_late[:], in_=product(0, last, BLOCKS))
-        nc.scalar.copy(out=second_late[:], in_=product(1, last, BLOCKS + 1))
+        first_late = shared.tile([P, VB, PACK], F32, name="first_late", offset=W3_AT, align_bytes=64)
+        second_late = shared.tile([P, VB, PACK], F32, name="second_late", offset=W3_AT + 2 * BLOCK_BYTES, align_bytes=64)
+        nc.scalar.copy(out=first_late[:], in_=product(0, LAST))
+        nc.scalar.copy(out=second_late[:], in_=product(1, LAST))
         pair.append(keep.tile([P, VB, PACK], F32, name="pair_3", tag="grouped_2", align_bytes=64))
-        nc.gpsimd.tensor_tensor(pair[last][:], second_late[:], first_late[:], MULT)
+        nc.gpsimd.tensor_tensor(pair[LAST][:], second_late[:], first_late[:], MULT)
 
         grouped4 = keep.tile([P, N, PACK], BF16, name="grouped4", align_bytes=64)
         codes4 = keep.tile([P, N], U32, name="codes4", align_bytes=64)
@@ -173,7 +185,7 @@ def tile_picked_trilin_relu_p_kernel(tc, x_words, x_scales, w1, w2, w3, w4, offs
         z = [keep.tile([P, VB, PACK], BF16, name="z_%d" % b, align_bytes=64) for b in range(BLOCKS)]
 
         def triple(b):
-            nc.vector.tensor_tensor(z[b][:], product(2, b, (0, 4, 5, 6)[b]), pair[b][:], MULT)
+            nc.vector.tensor_tensor(z[b][:], product(2, b), pair[b][:], MULT)
 
         def finish(b):
             z_codes = keep.tile([P, VB], U32, name="z_codes_%d" % b, align_bytes=64)
@@ -192,16 +204,16 @@ def tile_picked_trilin_relu_p_kernel(tc, x_words, x_scales, w1, w2, w3, w4, offs
                 )
 
             cols = slice(b * VB, (b + 1) * VB)
-            if b < last:
-                bank = psum.tile([P, PACK, VB], F32, name="out_bank_%d" % b, tag="bank_%d" % (1, 2, 3)[b])
+            if b < LAST:
+                bank = psum.tile([P, PACK, VB], F32, name="out_bank_%d" % b, tag="bank_%d" % OUT_BANKS[b])
                 for m in range(N // P):
                     output_rows(bank[:, m, :], m)
                 result = keep.tile([P, N // P, VB], F32, name="result_%d" % b)
                 nc.scalar.activation(result[:], bank[:, 0 : N // P, :], RELU)
                 nc.sync.dma_start(out=out[:, cols].rearrange("(m p) v -> p m v", p=P), in_=result[:])
             else:
-                upper = psum.tile([P, PACK, VB], F32, name="out_bank_upper", tag="bank_7")
-                lower = psum.tile([P, PACK, VB], F32, name="out_bank_lower", tag="bank_0")
+                upper = psum.tile([P, PACK, VB], F32, name="out_bank_upper", tag="bank_%d" % UPPER_BANK)
+                lower = psum.tile([P, PACK, VB], F32, name="out_bank_lower", tag="bank_%d" % LOWER_BANK)
                 output_rows(upper[:, 0, :], 0)
                 output_rows(lower[:, 0, :], 1)
                 result_upper = keep.tile([P, VB], F32, name="result_upper")
@@ -211,11 +223,11 @@ def tile_picked_trilin_relu_p_kernel(tc, x_words, x_scales, w1, w2, w3, w4, offs
                 nc.vector.tensor_scalar_max(result_lower[:], lower[:, 0, :], 0.0)
                 nc.sync.dma_start(out=out[P : 2 * P, cols], in_=result_lower[:])
 
-        for b in range(last):
+        for b in range(LAST):
             triple(b)
         nc.vector.quantize_mx(out=codes4[:].bitcast(FP8X4), scales=scales4[:], in_=grouped4[:].rearrange("p n t -> p (n t)"))
         finish(0)
         finish(1)
-        triple(last)
+        triple(LAST)
         finish(2)
-        finish(last)
+        finish(LAST)

@@ -26,14 +26,13 @@ SPREAD = P // (K // 32)
 VB = 128
 BLOCKS = V // VB
 LAST = BLOCKS - 1
-HALF = H // 2
 ROW0 = 4
-W3_SPLIT = H // (PACK * RUN) // 2
+W3_SPLIT = 16
+W2_CUTS = (0, 192, 384, H)
 
 BLOCK_BYTES = VB * PACK * 4
-W2_HIGH_AT = 0
+W2_AT = (9 * BLOCK_BYTES, 0, 3 * BLOCK_BYTES)
 W3_AT = 4 * BLOCK_BYTES
-W2_LOW_AT = 8 * BLOCK_BYTES
 
 FIRST_BANKS = (0, 1, 2, 4)
 SECOND_BANKS = (4, 5, 6, 5)
@@ -57,9 +56,10 @@ def tile_picked_trilin_relu_p_kernel(tc, x_words, x_scales, w1, w2, w3, w4, offs
         nc.sync.dma_start(offsets[:], offs)
         raw_w2 = {}
 
-        def load_w2_half(h):
-            raw_w2[h] = shared.tile([P, PACK, HALF], F32, name="raw_w2_%d" % h, offset=(W2_LOW_AT, W2_HIGH_AT)[h], align_bytes=64)
-            nc.sync.dma_start(out=raw_w2[h][:], in_=w2[:, h * HALF : (h + 1) * HALF].rearrange("(p j) c -> p j c", j=PACK))
+        def load_w2_part(h):
+            c0, c1 = W2_CUTS[h : h + 2]
+            raw_w2[h] = shared.tile([P, PACK, c1 - c0], F32, name="raw_w2_%d" % h, offset=W2_AT[h], align_bytes=64)
+            nc.sync.dma_start(out=raw_w2[h][:], in_=w2[:, c0:c1].rearrange("(p j) c -> p j c", j=PACK))
 
         raw_w1 = keep.tile([P, PACK, H], F32, name="raw_w1")
         w1_rows = w1.rearrange("(p j) c -> p j c", j=PACK)
@@ -72,10 +72,11 @@ def tile_picked_trilin_relu_p_kernel(tc, x_words, x_scales, w1, w2, w3, w4, offs
         picked_scales = keep.tile([P, S], U8, name="picked_scales", align_bytes=64)
         nc.vector.memset(picked_scales[:].bitcast(I32), 0)
         nc.vector.tensor_copy(spread_scales[:], table_scales[:].indirect(offsets[:]))
-        load_w2_half(0)
+        load_w2_part(0)
         for r in range(QUADRANT // SPREAD):
             nc.sync.dma_start(out=picked_scales[r:P:QUADRANT, :].bitcast(I32), in_=spread_scales[ROW0 + SPREAD * r : P : QUADRANT, :].bitcast(I32))
-        load_w2_half(1)
+        load_w2_part(1)
+        load_w2_part(2)
         raw_w3 = shared.tile([P, PACK, H], F32, name="raw_w3", offset=W3_AT, align_bytes=64)
         nc.sync.dma_start(out=raw_w3[:], in_=w3.rearrange("(p j) c -> p j c", j=PACK))
 
@@ -102,8 +103,8 @@ def tile_picked_trilin_relu_p_kernel(tc, x_words, x_scales, w1, w2, w3, w4, offs
                 in_=rows.rearrange("p j (u t e) -> p u t j e", t=PACK, e=RUN)[:, :, slots],
             )
 
-        def round_w2_half(copy, h, slots):
-            round_and_group(copy, grouped[1][:, :, h * HALF : (h + 1) * HALF], raw_w2[h][:], slots)
+        def round_w2_part(copy, h, slots):
+            round_and_group(copy, grouped[1][:, :, W2_CUTS[h] : W2_CUTS[h + 1]], raw_w2[h][:], slots)
 
         def quantize(d, t0=0, t1=PACK):
             cols = slice(t0 * P, t1 * P)
@@ -132,14 +133,17 @@ def tile_picked_trilin_relu_p_kernel(tc, x_words, x_scales, w1, w2, w3, w4, offs
         gather(0, words_01[:, 0:V])
         gather(1, words_01[:, V : 2 * V])
 
-        round_w2_half(nc.scalar.copy, 0, every)
-        round_w2_half(nc.vector.tensor_copy, 1, slice(0, PACK // 2))
-        round_w2_half(nc.scalar.copy, 1, slice(PACK // 2, PACK))
-        quantize(1)
+        low, high = slice(0, PACK // 2), slice(PACK // 2, PACK)
+        round_w2_part(nc.scalar.copy, 0, every)
+        round_w2_part(nc.scalar.copy, 1, every)
+        round_w2_part(nc.vector.tensor_copy, 2, low)
+        round_w2_part(nc.vector.tensor_copy, 2, high)
+        quantize(1, 0, PACK // 2)
+        quantize(1, PACK // 2, PACK)
 
-        words_2 = shared.tile([P, V], U32, name="picked_words_2", offset=W2_HIGH_AT, align_bytes=64)
+        words_2 = shared.tile([P, V], U32, name="picked_words_2", offset=W2_AT[2], align_bytes=64)
         gather(2, words_2[:])
-        first_early = shared.tile([P, LAST, VB, PACK], F32, name="first_early", offset=W2_HIGH_AT + BLOCK_BYTES, align_bytes=64)
+        first_early = shared.tile([P, LAST, VB, PACK], F32, name="first_early", offset=W2_AT[1], align_bytes=64)
         for b in range(LAST):
             nc.scalar.copy(out=first_early[:, b], in_=product(0, b))
         second = [product(1, b) for b in range(LAST)]
@@ -148,20 +152,19 @@ def tile_picked_trilin_relu_p_kernel(tc, x_words, x_scales, w1, w2, w3, w4, offs
         for b in range(2):
             nc.vector.tensor_tensor(pair[b][:], second[b], first_early[:, b], MULT)
 
-        round_and_group(nc.scalar.copy, grouped[2][:], raw_w3[:], slice(0, PACK // 2))
+        round_and_group(nc.scalar.copy, grouped[2][:], raw_w3[:], low)
         nc.scalar.copy(
-            out=grouped[2][:, 2].rearrange("p (u e j) -> p u j e", e=RUN, j=PACK)[:, 0:W3_SPLIT],
-            in_=raw_w3[:].rearrange("p j (u t e) -> p t u j e", t=PACK, e=RUN)[:, 2, 0:W3_SPLIT],
+            out=grouped[2][:, high].rearrange("p t (u e j) -> p u t j e", e=RUN, j=PACK)[:, 0:W3_SPLIT],
+            in_=raw_w3[:].rearrange("p j (u t e) -> p u t j e", t=PACK, e=RUN)[:, 0:W3_SPLIT, high],
         )
-        for t, u0 in ((3, 0), (2, W3_SPLIT)):
-            nc.gpsimd.tensor_scalar(
-                grouped[2][:, t].rearrange("p (u e j) -> p u j e", e=RUN, j=PACK)[:, u0:],
-                raw_w3[:].rearrange("p j (u t e) -> p t u j e", t=PACK, e=RUN)[:, t, u0:],
-                1.0,
-                0.0,
-                MULT,
-                ADD,
-            )
+        nc.gpsimd.tensor_scalar(
+            grouped[2][:, high].rearrange("p t (u e j) -> p u t e j", e=RUN, j=PACK)[:, W3_SPLIT:],
+            raw_w3[:].rearrange("p j (u t e) -> p u t e j", t=PACK, e=RUN)[:, W3_SPLIT:, high],
+            1.0,
+            0.0,
+            MULT,
+            ADD,
+        )
         quantize(2, 0, PACK // 2)
         quantize(2, PACK // 2, PACK)
 

@@ -18,7 +18,7 @@ RELU = mybir.ActivationFunctionType.Relu
 
 P = 128
 PACK = 4
-RUN = 2
+RUN = 4
 PIECES = 3
 LIST_ROWS = 16
 QUADRANT = 32
@@ -27,7 +27,7 @@ VB = 128
 BLOCKS = V // VB
 LAST = BLOCKS - 1
 ROW0 = 4
-W3_SPLIT = 16
+W3_SPLIT = 8
 W2_CUTS = (0, 192, 384, H)
 
 BLOCK_BYTES = VB * PACK * 4

@@ -26,6 +26,8 @@ SPREAD = P // (K // 32)
 VB = 128
 BLOCKS = V // VB
 LAST = BLOCKS - 1
+TWO = 2
+WALK = [P, VB // TWO, PACK, TWO]
 ROW0 = 4
 W3_SPLIT = 8
 W2_CUTS = (0, 192, 384, H)
@@ -122,7 +124,7 @@ def tile_picked_trilin_relu_p_kernel(tc, x_words, x_scales, w1, w2, w3, w4, offs
                     start=True,
                     stop=True,
                 )
-            return bank[:].rearrange("p t v -> p v t")
+            return bank[:].rearrange("p t (v e) -> p v t e", e=TWO)
 
         warm = keep.tile([P, 1], F32, name="warm")
         nc.scalar.activation(warm[:], raw_w1[:, 0, 0:1], RELU)
@@ -143,12 +145,12 @@ def tile_picked_trilin_relu_p_kernel(tc, x_words, x_scales, w1, w2, w3, w4, offs
 
         words_2 = shared.tile([P, V], U32, name="picked_words_2", offset=W2_AT[2], align_bytes=64)
         gather(2, words_2[:])
-        first_early = shared.tile([P, LAST, VB, PACK], F32, name="first_early", offset=W2_AT[1], align_bytes=64)
+        first_early = shared.tile([P, LAST, *WALK[1:]], F32, name="first_early", offset=W2_AT[1], align_bytes=64)
         for b in range(LAST):
             nc.scalar.copy(out=first_early[:, b], in_=product(0, b))
         second = [product(1, b) for b in range(LAST)]
 
-        pair = [keep.tile([P, VB, PACK], F32, name="pair_%d" % b) for b in range(2)]
+        pair = [keep.tile(WALK, F32, name="pair_%d" % b) for b in range(2)]
         for b in range(2):
             nc.vector.tensor_tensor(pair[b][:], second[b], first_early[:, b], MULT)
 
@@ -168,13 +170,13 @@ def tile_picked_trilin_relu_p_kernel(tc, x_words, x_scales, w1, w2, w3, w4, offs
         quantize(2, 0, PACK // 2)
         quantize(2, PACK // 2, PACK)
 
-        pair.append(shared.tile([P, VB, PACK], F32, name="pair_2", offset=W3_AT + BLOCK_BYTES, align_bytes=64))
+        pair.append(shared.tile(WALK, F32, name="pair_2", offset=W3_AT + BLOCK_BYTES, align_bytes=64))
         nc.vector.tensor_tensor(pair[2][:], second[2], first_early[:, 2], MULT)
-        first_late = shared.tile([P, VB, PACK], F32, name="first_late", offset=W3_AT, align_bytes=64)
-        second_late = shared.tile([P, VB, PACK], F32, name="second_late", offset=W3_AT + 2 * BLOCK_BYTES, align_bytes=64)
+        first_late = shared.tile(WALK, F32, name="first_late", offset=W3_AT, align_bytes=64)
+        second_late = shared.tile(WALK, F32, name="second_late", offset=W3_AT + 2 * BLOCK_BYTES, align_bytes=64)
         nc.scalar.copy(out=first_late[:], in_=product(0, LAST))
         nc.scalar.copy(out=second_late[:], in_=product(1, LAST))
-        pair.append(keep.tile([P, VB, PACK], F32, name="pair_3", tag="grouped_2", align_bytes=64))
+        pair.append(keep.tile(WALK, F32, name="pair_3", tag="grouped_2", align_bytes=64))
         nc.gpsimd.tensor_tensor(pair[LAST][:], second_late[:], first_late[:], MULT)
 
         grouped4 = keep.tile([P, N, PACK], BF16, name="grouped4", align_bytes=64)
@@ -188,7 +190,7 @@ def tile_picked_trilin_relu_p_kernel(tc, x_words, x_scales, w1, w2, w3, w4, offs
         z = [keep.tile([P, VB, PACK], BF16, name="z_%d" % b, align_bytes=64) for b in range(BLOCKS)]
 
         def triple(b):
-            nc.vector.tensor_tensor(z[b][:], product(2, b), pair[b][:], MULT)
+            nc.vector.tensor_tensor(z[b][:].rearrange("p (v e) t -> p v t e", e=TWO), product(2, b), pair[b][:], MULT)
 
         def finish(b):
             z_codes = keep.tile([P, VB], U32, name="z_codes_%d" % b, align_bytes=64)

from contextlib import ExitStack

import concourse.mybir as mybir

K, T, S, V, H, N = 512, 4096, 1536, 512, 512, 256
FLOPS = 2 * K * H * S + 2 * H * N * V

F32 = mybir.dt.float32
BF16 = mybir.dt.bfloat16
I32 = mybir.dt.int32
U32 = mybir.dt.uint32
U16 = mybir.dt.uint16
U8 = mybir.dt.uint8
FP8X4 = mybir.dt.float8_e4m3fn_x4
MULT = mybir.AluOpType.mult
ADD = mybir.AluOpType.add
RELU = mybir.ActivationFunctionType.Relu

P = 128
PACK = 4
RUN = 4
PIECES = 3
LIST_ROWS = 16
QUADRANT = 32
SPREAD = P // (K // 32)
VB = 128
BLOCKS = V // VB
LAST = BLOCKS - 1
TWO = 2
WALK = [P, VB // TWO, PACK, TWO]
ROW0 = 4
W3_SPLIT = 8
W2_CUTS = (0, 192, 384, H)

BLOCK_BYTES = VB * PACK * 4
W2_AT = (9 * BLOCK_BYTES, 0, 3 * BLOCK_BYTES)
W3_AT = 4 * BLOCK_BYTES

FIRST_BANKS = (0, 1, 2, 4)
SECOND_BANKS = (4, 5, 6, 5)
THIRD_BANKS = (0, 4, 5, 6)
OUT_BANKS = (1, 2, 3)
UPPER_BANK, LOWER_BANK = 7, 0


def tile_picked_trilin_relu_p_kernel(tc, x_words, x_scales, w1, w2, w3, w4, offs, out):
    nc = tc.nc
    with ExitStack() as ctx:
        keep = ctx.enter_context(tc.tile_pool(name="keep", bufs=1))
        shared = ctx.enter_context(tc.tile_pool(name="shared", bufs=1))
        psum = ctx.enter_context(tc.psum_pool(name="psum", bufs=1))

        offsets = keep.tile([P, S // LIST_ROWS], U16, name="offsets")
        table_words = keep.tile([P, T], I32, name="table_words", align_bytes=64)
        table_scales = keep.tile([P, T], U8, name="table_scales", tag="scales_then_words", align_bytes=64)

        nc.vector.memset(table_scales[:].bitcast(I32), 0)
        nc.sync.dma_start(offsets[:], offs)
        raw_w2 = {}

        def load_w2_part(h):
            c0, c1 = W2_CUTS[h : h + 2]
            raw_w2[h] = shared.tile([P, PACK, c1 - c0], F32, name="raw_w2_%d" % h, offset=W2_AT[h], align_bytes=64)
            nc.sync.dma_start(out=raw_w2[h][:], in_=w2[:, c0:c1].rearrange("(p j) c -> p j c", j=PACK))

        raw_w1 = keep.tile([P, PACK, H], F32, name="raw_w1")
        w1_rows = w1.rearrange("(p j) c -> p j c", j=PACK)
        nc.sync.dma_start(out=raw_w1[:, 0 : PACK // 2, :], in_=w1_rows[:, 0 : PACK // 2, :])
        nc.sync.dma_start(out=table_scales[ROW0:P:SPREAD, :].bitcast(I32), in_=x_scales[0].bitcast(I32))
        nc.sync.dma_start(out=raw_w1[:, PACK // 2 : PACK, :], in_=w1_rows[:, PACK // 2 : PACK, :])
        nc.sync.dma_start(out=table_words[:], in_=x_words[0].rearrange("p c r -> p (c r)").bitcast(I32))

        spread_scales = keep.tile([P, S], U8, name="spread_scales", align_bytes=64)
        picked_scales = keep.tile([P, S], U8, name="picked_scales", align_bytes=64)
        nc.vector.memset(picked_scales[:].bitcast(I32), 0)
        nc.vector.tensor_copy(spread_scales[:], table_scales[:].indirect(offsets[:]))
        load_w2_part(0)
        for r in range(QUADRANT // SPREAD):
            nc.sync.dma_start(out=picked_scales[r:P:QUADRANT, :].bitcast(I32), in_=spread_scales[ROW0 + SPREAD * r : P : QUADRANT, :].bitcast(I32))
        load_w2_part(1)
        load_w2_part(2)
        raw_w3 = shared.tile([P, PACK, H], F32, name="raw_w3", offset=W3_AT, align_bytes=64)
        nc.sync.dma_start(out=raw_w3[:], in_=w3.rearrange("(p j) c -> p j c", j=PACK))

        raw4 = keep.tile([P, PACK, N], F32, name="raw4")
        w4_rows = w4.rearrange("(u t e) n -> t u e n", t=PACK, e=RUN)
        for t in range(PACK):
            nc.sync.dma_start(out=raw4[:, t, :], in_=w4_rows[t])

        picked_words = {}

        def gather(d, into):
            nc.vector.tensor_copy(into, table_words[:].bitcast(U32).indirect(offsets[:, d * V // LIST_ROWS : (d + 1) * V // LIST_ROWS]))
            picked_words[d] = into

        words_01 = keep.tile([P, 2 * V], U32, name="picked_words_01", tag="scales_then_words", align_bytes=64)

        grouped = [keep.tile([P, PACK, P * PACK], BF16, name="grouped_%d" % d, tag="grouped_%d" % d, align_bytes=64) for d in range(PIECES)]
        codes = [keep.tile([P, H], U32, name="codes_%d" % d, align_bytes=64) for d in range(PIECES)]
        scales = [keep.tile([P, H], U8, name="scales_%d" % d, align_bytes=64) for d in range(PIECES)]

        def round_and_group(copy, into, rows, slots):
            copy(
                out=into[:, slots].rearrange("p t (u e j) -> p u t j e", e=RUN, j=PACK),
                in_=rows.rearrange("p j (u t e) -> p u t j e", t=PACK, e=RUN)[:, :, slots],
            )

        def round_w2_part(copy, h, slots):
            round_and_group(copy, grouped[1][:, :, W2_CUTS[h] : W2_CUTS[h + 1]], raw_w2[h][:], slots)

        def quantize(d, t0=0, t1=PACK):
            cols = slice(t0 * P, t1 * P)
            nc.vector.quantize_mx(out=codes[d][:, cols].bitcast(FP8X4), scales=scales[d][:, cols], in_=grouped[d][:, t0:t1].rearrange("p t c -> p (t c)"))

        def product(d, b):
            bank = psum.tile([P, PACK, VB], F32, name="bank_%d_%d" % (d, b), tag="bank_%d" % (FIRST_BANKS, SECOND_BANKS, THIRD_BANKS)[d][b])
            for t in range(PACK):
                nc.tensor.matmul_mx(
                    out=bank[:, t, :],
                    lhsT=codes[d][:, t * P : (t + 1) * P].bitcast(FP8X4),
                    lhsT_scale=scales[d][:, t * P : (t + 1) * P],
                    rhs=picked_words[d][:, b * VB : (b + 1) * VB].bitcast(FP8X4),
                    rhs_scale=picked_scales[:, d * V + b * VB : d * V + (b + 1) * VB],
                    start=True,
                    stop=True,
                )
            return bank[:].rearrange("p t (v e) -> p v t e", e=TWO)

        warm = keep.tile([P, 1], F32, name="warm")
        nc.scalar.activation(warm[:], raw_w1[:, 0, 0:1], RELU)

        every = slice(0, PACK)
        round_and_group(nc.scalar.copy, grouped[0][:], raw_w1[:], every)
        quantize(0)
        gather(0, words_01[:, 0:V])
        gather(1, words_01[:, V : 2 * V])

        low, high = slice(0, PACK // 2), slice(PACK // 2, PACK)
        round_w2_part(nc.scalar.copy, 0, every)
        round_w2_part(nc.scalar.copy, 1, every)
        round_w2_part(nc.vector.tensor_copy, 2, low)
        round_w2_part(nc.vector.tensor_copy, 2, high)
        quantize(1, 0, PACK // 2)
        quantize(1, PACK // 2, PACK)

        words_2 = shared.tile([P, V], U32, name="picked_words_2", offset=W2_AT[2], align_bytes=64)
        gather(2, words_2[:])
        first_early = shared.tile([P, LAST, *WALK[1:]], F32, name="first_early", offset=W2_AT[1], align_bytes=64)
        for b in range(LAST):
            nc.scalar.copy(out=first_early[:, b], in_=product(0, b))
        second = [product(1, b) for b in range(LAST)]

        pair = [keep.tile(WALK, F32, name="pair_%d" % b) for b in range(2)]
        for b in range(2):
            nc.vector.tensor_tensor(pair[b][:], second[b], first_early[:, b], MULT)

        round_and_group(nc.scalar.copy, grouped[2][:], raw_w3[:], low)
        nc.scalar.copy(
            out=grouped[2][:, high].rearrange("p t (u e j) -> p u t j e", e=RUN, j=PACK)[:, 0:W3_SPLIT],
            in_=raw_w3[:].rearrange("p j (u t e) -> p u t j e", t=PACK, e=RUN)[:, 0:W3_SPLIT, high],
        )
        nc.gpsimd.tensor_scalar(
            grouped[2][:, high].rearrange("p t (u e j) -> p u t e j", e=RUN, j=PACK)[:, W3_SPLIT:],
            raw_w3[:].rearrange("p j (u t e) -> p u t e j", t=PACK, e=RUN)[:, W3_SPLIT:, high],
            1.0,
            0.0,
            MULT,
            ADD,
        )
        quantize(2, 0, PACK // 2)
        quantize(2, PACK // 2, PACK)

        pair.append(shared.tile(WALK, F32, name="pair_2", offset=W3_AT + BLOCK_BYTES, align_bytes=64))
        nc.vector.tensor_tensor(pair[2][:], second[2], first_early[:, 2], MULT)
        first_late = shared.tile(WALK, F32, name="first_late", offset=W3_AT, align_bytes=64)
        second_late = shared.tile(WALK, F32, name="second_late", offset=W3_AT + 2 * BLOCK_BYTES, align_bytes=64)
        nc.scalar.copy(out=first_late[:], in_=product(0, LAST))
        nc.scalar.copy(out=second_late[:], in_=product(1, LAST))
        pair.append(keep.tile(WALK, F32, name="pair_3", tag="grouped_2", align_bytes=64))
        nc.gpsimd.tensor_tensor(pair[LAST][:], second_late[:], first_late[:], MULT)

        grouped4 = keep.tile([P, N, PACK], BF16, name="grouped4", align_bytes=64)
        codes4 = keep.tile([P, N], U32, name="codes4", align_bytes=64)
        scales4 = keep.tile([P, N], U8, name="scales4", align_bytes=64)
        nc.scalar.copy(
            out=grouped4[:].rearrange("p (c e) t -> p c t e", e=RUN),
            in_=raw4[:].rearrange("p t (c e) -> p c t e", e=RUN),
        )

        z = [keep.tile([P, VB, PACK], BF16, name="z_%d" % b, align_bytes=64) for b in range(BLOCKS)]

        def triple(b):
            nc.vector.tensor_tensor(z[b][:].rearrange("p (v e) t -> p v t e", e=TWO), product(2, b), pair[b][:], MULT)

        def finish(b):
            z_codes = keep.tile([P, VB], U32, name="z_codes_%d" % b, align_bytes=64)
            z_scales = keep.tile([P, VB], U8, name="z_scales_%d" % b, align_bytes=64)
            nc.vector.quantize_mx(out=z_codes[:].bitcast(FP8X4), scales=z_scales[:], in_=z[b][:].rearrange("p v t -> p (v t)"))

            def output_rows(into, m):
                nc.tensor.matmul_mx(
                    out=into,
                    lhsT=codes4[:, m * P : (m + 1) * P].bitcast(FP8X4),
                    lhsT_scale=scales4[:, m * P : (m + 1) * P],
                    rhs=z_codes[:].bitcast(FP8X4),
                    rhs_scale=z_scales[:],
                    start=True,
                    stop=True,
                )

            cols = slice(b * VB, (b + 1) * VB)
            if b < LAST:
                bank = psum.tile([P, PACK, VB], F32, name="out_bank_%d" % b, tag="bank_%d" % OUT_BANKS[b])
                for m in range(N // P):
                    output_rows(bank[:, m, :], m)
                result = keep.tile([P, N // P, VB], F32, name="result_%d" % b)
                nc.scalar.activation(result[:], bank[:, 0 : N // P, :], RELU)
                nc.sync.dma_start(out=out[:, cols].rearrange("(m p) v -> p m v", p=P), in_=result[:])
            else:
                upper = psum.tile([P, PACK, VB], F32, name="out_bank_upper", tag="bank_%d" % UPPER_BANK)
                lower = psum.tile([P, PACK, VB], F32, name="out_bank_lower", tag="bank_%d" % LOWER_BANK)
                output_rows(upper[:, 0, :], 0)
                output_rows(lower[:, 0, :], 1)
                result_upper = keep.tile([P, VB], F32, name="result_upper")
                result_lower = keep.tile([P, VB], F32, name="result_lower")
                nc.scalar.activation(result_upper[:], upper[:, 0, :], RELU)
                nc.scalar.dma_start(out=out[0:P, cols], in_=result_upper[:])
                nc.vector.tensor_scalar_max(result_lower[:], lower[:, 0, :], 0.0)
                nc.sync.dma_start(out=out[P : 2 * P, cols], in_=result_lower[:])

        for b in range(LAST):
            triple(b)
        nc.vector.quantize_mx(out=codes4[:].bitcast(FP8X4), scales=scales4[:], in_=grouped4[:].rearrange("p n t -> p (n t)"))
        finish(0)
        finish(1)
        triple(LAST)
        finish(2)
        finish(LAST)
